import numpy as np
import ml_dtypes


def mxq(x, axis, fmt="e4m3"):
    dtype, down = {"e4m3": (ml_dtypes.float8_e4m3fn, 7), "e5m2": (ml_dtypes.float8_e5m2, 14)}[fmt]
    v = np.moveaxis(np.asarray(x, np.float32).astype(ml_dtypes.bfloat16).astype(np.float64), axis, -1)
    blocks = v.reshape(v.shape[:-1] + (-1, 32))
    amax = np.abs(blocks).max(-1, keepdims=True)
    byte = np.maximum(np.where(amax > 0, np.frexp(amax)[1] - 1 + 127, 0) - down, 1)
    scale = np.exp2(byte - 127.0)
    codes = (blocks / scale).astype(np.float32).astype(dtype).astype(np.float64)
    return np.moveaxis((codes * scale).reshape(v.shape), -1, axis)


WIDE = False


def mx_kscale(k):
    if not WIDE:
        return np.ones(k)
    levels = np.array([10, -10, 5, -5, 0])
    if k % 512:
        return np.exp2(np.random.permutation(np.resize(levels, k // 32))).repeat(32)
    a = np.empty((k // 512, 16))
    for p in range(k // 512):
        a[p, :8] = np.random.permutation(np.resize(levels, 8))
        for g in range(8):
            far = levels[np.abs(levels - a[p, g]) >= 10]
            a[p, g + 8] = far[np.random.randint(len(far))]
    return np.exp2(a.ravel()).repeat(32)


BF16 = ml_dtypes.bfloat16


def bf(x):
    return np.asarray(x, np.float32).astype(BF16)


def f64(x):
    return np.asarray(x).astype(np.float64)

def planes(Y):
    n, m = Y.shape
    b = f64(bf(Y)).reshape(n // 32, 32, m)
    amax = np.abs(b).max(1)
    byte = np.clip(np.where(amax > 0, np.frexp(amax)[1] - 1 + 127 - 7, 1), 1, 254)
    codes = (b * np.exp2(127.0 - byte)[:, None, :]).reshape(n, m).astype(np.float32).astype(ml_dtypes.float8_e4m3fn).view(np.uint8)
    words = codes.reshape(n // 512, 128, 4, m).transpose(0, 1, 3, 2)
    return np.ascontiguousarray(words), np.ascontiguousarray(byte.astype(np.uint8).reshape(n // 512, 16, m))


R, S, T, F, A = 4, 1024, 512, 512, 1024

def setup_inputs():
    st = mx_kscale(T)
    ss = mx_kscale(S)
    rn = np.random.randn
    scale = 0.8 * np.exp(0.8 * rn(A))
    return {
        "history": bf(rn(R, S, T) * st),
        "encoder": bf(rn(T, F) / np.sqrt(T) / st[:, None]),
        "sensor_gain": bf((1.0 + 0.1 * rn(S)) * ss),
        "policy": bf(rn(S, A) / np.sqrt(S) / ss[:, None]),
        "policy_bias": bf(0.3 * rn(A)),
        "action_scale": bf(scale),
        "pose_offset": bf(0.3 * rn(R, A) * scale),
    }

def reference(history, encoder, sensor_gain, policy, policy_bias, action_scale, pose_offset):
    hq = mxq(f64(history), 2, "e4m3")
    eq = mxq(f64(encoder), 0, "e4m3")
    Z = hq @ eq
    elu = np.maximum(Z, 0.0) + np.exp(np.minimum(Z, 0.0)) - 1.0
    H = elu * f64(sensor_gain)[None, :, None]
    Hq = mxq(H, 1, "e4m3")
    pq = mxq(f64(policy), 0, "e4m3")
    U = Hq.swapaxes(1, 2) @ pq
    y = np.tanh(U + f64(policy_bias)) * f64(action_scale) + f64(pose_offset)[:, None, :]
    Y = y.reshape(R * F, A).T
    words, scales = planes(Y)
    return y, words, scales

@@ -1,0 +1,406 @@
+from contextlib import ExitStack
+
+import concourse.mybir as mybir
+from concourse.masks import make_identity
+
+R, S, T, F, A = 4, 1024, 512, 512, 1024
+FLOPS = 2 * R * S * T * F + 2 * R * F * S * A
+
+F32 = mybir.dt.float32
+BF16 = mybir.dt.bfloat16
+U32 = mybir.dt.uint32
+I32 = mybir.dt.int32
+U8 = mybir.dt.uint8
+FP8X4 = mybir.dt.float8_e4m3fn_x4
+ACT = mybir.ActivationFunctionType
+ALU = mybir.AluOpType
+ENGINE = mybir.EngineType
+
+P = 128
+PACK = 4
+GROUP = P * PACK
+NG = 2
+HALF = GROUP // 2
+BANKS = R * NG * PACK
+
+ROW_OFFSET, ROW_GAIN, ROW_BIAS, ROW_SCALE, ROWS = 0, 8, 10, 12, 14
+
+STAGE2_LAG = 10
+TURN_LAG = STAGE2_LAG + 6
+PINNED_FROM = 4
+VECTOR_FREE_FROM = 22
+LAST_GROUP = BANKS - PACK
+
+
+def tile_legged_action_chunk_planes_h3_kernel(
+    tc, history, encoder, sensor_gain, policy, policy_bias, action_scale, pose_offset, out_0, out_1, out_2
+):
+    nc = tc.nc
+    with ExitStack() as ctx:
+        keep = ctx.enter_context(tc.tile_pool(name="keep", bufs=1))
+        work = ctx.enter_context(tc.tile_pool(name="work", bufs=2))
+        psum = ctx.enter_context(tc.psum_pool(name="psum", bufs=1))
+
+        def z_pool_bank(shape):
+            return psum.tile(shape, F32, tag="z", name="z", bufs=3)
+
+        def u_pool_bank(shape):
+            return psum.tile(shape, F32, tag="u", name="u", bufs=2)
+
+        def turn_pool_bank(shape):
+            return psum.tile(shape, F32, tag="turn", name="turn", bufs=3)
+
+        def quantize(codes, scales, values):
+            nc.vector.quantize_mx(out=codes.bitcast(FP8X4), scales=scales, in_=values)
+
+        def mx_matmul(out, lhs_codes, lhs_scales, rhs_codes, rhs_scales, start, stop):
+            nc.tensor.matmul_mx(out=out, lhsT=lhs_codes.bitcast(FP8X4), lhsT_scale=lhs_scales,
+                                rhs=rhs_codes.bitcast(FP8X4), rhs_scale=rhs_scales, start=start, stop=stop)
+
+        hist_raw, pol_raw = {}, {}
+        enc_raw = keep.tile([P, PACK, F], BF16)
+        rows_bf = keep.tile([P, GROUP], BF16)
+
+        def history_rows(n):
+            r, g = divmod(n, NG)
+            return history[r, g * GROUP:(g + 1) * GROUP, :].rearrange("(m t) k -> m t k", t=PACK)
+
+        def load_history(n):
+            raw = keep.tile([P, PACK, T], BF16, name="hist_%d" % n)
+            nc.sync.dma_start(out=raw[:], in_=history_rows(n))
+            for h in range(2):
+                hist_raw[n, h] = raw[:, 2 * h:2 * h + 2, :]
+
+        def load_policy(n):
+            ag, g = divmod(n, NG)
+            pol_raw[n] = keep.tile([P, PACK, GROUP], BF16, name="pol_%d" % n)
+            block = policy[g * GROUP:(g + 1) * GROUP, ag * GROUP:(ag + 1) * GROUP]
+            nc.sync.dma_start(out=pol_raw[n][:], in_=block.rearrange("(p j) a -> p j a", j=PACK))
+
+        def load_inputs():
+            load_policy(0)
+            for h in range(2):
+                raw = keep.tile([P, 2, T], BF16, name="hist_0_%d" % h)
+                nc.sync.dma_start(out=raw[:], in_=history_rows(0)[:, 2 * h:2 * h + 2, :])
+                hist_raw[0, h] = raw[:]
+            nc.sync.dma_start(out=enc_raw[:], in_=encoder.rearrange("(p j) f -> p j f", j=PACK))
+            nc.sync.dma_start(out=rows_bf[ROW_OFFSET:ROW_OFFSET + R * NG, :],
+                              in_=pose_offset.rearrange("r (g c) -> (r g) c", g=NG))
+            for row, vec in ((ROW_GAIN, sensor_gain), (ROW_BIAS, policy_bias), (ROW_SCALE, action_scale)):
+                nc.sync.dma_start(out=rows_bf[row:row + NG, :], in_=vec.rearrange("(g c) -> g c", g=NG))
+            for n in range(1, R * NG):
+                if n < NG * NG:
+                    load_policy(n)
+                load_history(n)
+
+        ident = keep.tile([P, P], F32)
+        rows_f = keep.tile([P, GROUP], F32)
+        table_load = keep.tile([P, 1], F32)
+        chan = keep.tile([P, ROWS, PACK], F32)
+        one_values = keep.tile([P, P * PACK], BF16, align_bytes=64)
+        one_codes = keep.tile([P, P], U32, align_bytes=64)
+        one_scales = keep.tile([P, P], U8, align_bytes=64)
+        frac_values = keep.tile([P, GROUP * PACK], BF16, align_bytes=64)
+        frac_codes = keep.tile([P, GROUP], U32, align_bytes=64)
+        frac_scales = keep.tile([P, GROUP], U8, align_bytes=64)
+
+        def make_constants():
+            make_identity(nc, ident[:])
+            nc.vector.memset(rows_f[:], 0.0)
+            nc.scalar.activation(out=table_load[:], in_=rows_f[:, 0:1], func=ACT.Exp)
+            nc.vector.memset(one_values[:], 1.0)
+            nc.vector.memset(frac_values[:], 1.0 / GROUP)
+            quantize(one_codes[:], one_scales[:], one_values[:])
+            quantize(frac_codes[:], frac_scales[:], frac_values[:])
+
+        def channel_rows():
+            nc.scalar.copy(out=rows_f[0:ROWS, :].rearrange("q (t p) -> q t p", t=PACK),
+                           in_=rows_bf[0:ROWS, :].rearrange("q (p t) -> q t p", t=PACK))
+
+        def channel_columns():
+            bank = u_pool_bank([P, P, PACK])
+            for t in range(PACK):
+                nc.tensor.transpose(bank[:, :, t], rows_f[:, t * P:(t + 1) * P], ident[:])
+            nc.scalar.copy(out=chan[:], in_=bank[:, 0:ROWS, :])
+
+        def column(row, t):
+            return chan[:, row, t:t + 1]
+
+        enc_grouped = keep.tile([P, F, PACK], BF16, align_bytes=64)
+        enc_codes = keep.tile([P, F], U32, align_bytes=64)
+        enc_scales = keep.tile([P, F], U8, align_bytes=64)
+
+        def interleave(dst, src):
+            nc.vector.tensor_copy(out=dst.rearrange("p (c i) t -> p c t i", i=4),
+                                  in_=src.rearrange("p t (c i) -> p c t i", i=4))
+
+        def encoder_interleave(h):
+            cols = slice(h * HALF, (h + 1) * HALF)
+            interleave(enc_grouped[:, cols, :], enc_raw[:, :, cols])
+
+        def encoder_quantize(h):
+            cols = slice(h * HALF, (h + 1) * HALF)
+            quantize(enc_codes[:, cols], enc_scales[:, cols], enc_grouped[:, cols, :].rearrange("p f j -> p (f j)"))
+
+        hist_bank, hist_grouped, hist_codes, hist_scales = {}, {}, {}, {}
+
+        def history_transpose(n, h):
+            bank = turn_pool_bank([P, 2, 2, P])
+            for t in range(2):
+                words = hist_raw[n, h][:, t, :].bitcast(F32)
+                for u in range(2):
+                    nc.tensor.transpose(bank[:, t, u, :], words[:, u:T // 2:2], ident[:])
+            hist_bank[n, h] = bank
+
+        def history_copy(n, h):
+            if h == 0:
+                hist_grouped[n] = work.tile([P, 2, 2 * P * PACK], BF16, tag="hist_grouped", name="hist_grouped",
+                                            bufs=5, align_bytes=64)
+            nc.scalar.copy(out=hist_grouped[n][:, h, :].bitcast(F32).rearrange("p (t m u) -> p t m u", t=2, u=2),
+                           in_=hist_bank[n, h][:].rearrange("p t u m -> p t m u"))
+
+        def history_quantize(n, first, last):
+            if first == 0:
+                hist_codes[n] = keep.tile([P, GROUP], U32, name="hist_codes_%d" % n, align_bytes=64)
+                hist_scales[n] = keep.tile([P, GROUP], U8, name="hist_scales_%d" % n, align_bytes=64)
+            cols = slice(first * HALF, last * HALF)
+            quantize(hist_codes[n][:, cols], hist_scales[n][:, cols],
+                     hist_grouped[n][:, first:last, :].rearrange("p h c -> p (h c)"))
+
+        pol_codes = keep.tile([P, NG, A], U32, align_bytes=64)
+        pol_scales = keep.tile([P, NG, A], U8, align_bytes=64)
+        pol_grouped = {}
+
+        def policy_interleave(n, h):
+            if h == 0:
+                pol_grouped[n] = work.tile([P, PACK, P, PACK], BF16, tag="pol_grouped", name="pol_grouped",
+                                           align_bytes=64)
+            dst = pol_grouped[n][:, 2 * h:2 * h + 2, :, :]
+            src = pol_raw[n][:].rearrange("p j (m t) -> p t m j", t=PACK)[:, 2 * h:2 * h + 2, :, :]
+            if h == 1 and n < NG:
+                nc.vector.tensor_copy(out=dst, in_=src)
+            else:
+                nc.scalar.copy(out=dst, in_=src)
+
+        def policy_quantize(n):
+            ag, g = divmod(n, NG)
+            cols = slice(ag * GROUP, (ag + 1) * GROUP)
+            quantize(pol_codes[:, g, cols], pol_scales[:, g, cols], pol_grouped[n][:].rearrange("p t m j -> p (t m j)"))
+
+        z_bank, exp_z, elu_one, h_grouped, h_codes, h_scales = {}, {}, {}, {}, {}, {}
+
+        def z_matmul(i):
+            n, chunk = divmod(i, PACK)
+            bank = z_pool_bank([P, PACK, P])
+            mx_matmul(bank[:].rearrange("p t f -> p (t f)"), one_codes[:], one_scales[:], frac_codes[:], frac_scales[:],
+                      True, False)
+            fcols = slice(chunk * P, (chunk + 1) * P)
+            for t in range(PACK):
+                scols = slice(t * P, (t + 1) * P)
+                mx_matmul(bank[:, t, :], hist_codes[n][:, scols], hist_scales[n][:, scols],
+                          enc_codes[:, fcols], enc_scales[:, fcols], False, t == PACK - 1)
+            z_bank[i] = bank[:].rearrange("p t f -> p f t")
+
+        def z_exp(i):
+            exp_z[i] = work.tile([P, P, PACK], F32, tag="exp_z", name="exp_z", bufs=3)
+            nc.scalar.activation(out=exp_z[i][:], in_=z_bank[i], func=ACT.Exp, bias=-1.0)
+
+        def z_max(i):
+            pair, k = divmod(i, 2)
+            if k == 0:
+                elu_one[pair] = work.tile([P, 2 * P, PACK], F32, tag="elu_one", name="elu_one")
+            nc.vector.scalar_tensor_tensor(out=elu_one[pair][:, k * P:(k + 1) * P, :], in0=exp_z[i][:], scalar=1.0,
+                                           in1=z_bank[i], op0=ALU.min, op1=ALU.max)
+
+        def z_gain(pair):
+            n, h = divmod(pair, 2)
+            if h == 0:
+                h_grouped[n] = work.tile([P, F, PACK], BF16, tag="h_grouped", name="h_grouped", align_bytes=64)
+            row = ROW_GAIN + n % NG
+            nc.vector.scalar_tensor_tensor(out=h_grouped[n][:, h * HALF:(h + 1) * HALF, :], in0=elu_one[pair][:],
+                                           scalar=-1.0, in1=chan[:, row:row + 1, :].to_broadcast([P, HALF, PACK]),
+                                           op0=ALU.add, op1=ALU.mult)
+
+        def h_quantize(n):
+            h_codes[n] = work.tile([P, F], U32, tag="h_codes", name="h_codes", bufs=4, align_bytes=64)
+            h_scales[n] = work.tile([P, F], U8, tag="h_scales", name="h_scales", bufs=4, align_bytes=64)
+            quantize(h_codes[n][:], h_scales[n][:], h_grouped[n][:].rearrange("p f t -> p (f t)"))
+
+        u_bank, tanh_u, y_slots, y_grouped, y_codes, y_bank, y_rows = {}, {}, {}, {}, {}, {}, {}
+        y_scales = keep.tile([P, R * F], U8, align_bytes=64)
+        words_out = out_1.rearrange("g p m t -> g p (m t)").bitcast(I32)
+        scales_out = out_2.bitcast(I32)
+
+        def u_matmul(j):
+            n, t = divmod(j, PACK)
+            r, ag = divmod(n, NG)
+            bank = z_pool_bank([P, F]) if j > LAST_GROUP else u_pool_bank([P, F])
+            acols = slice(ag * GROUP + t * P, ag * GROUP + (t + 1) * P)
+            for g in range(NG):
+                mx_matmul(bank[:], pol_codes[:, g, acols], pol_scales[:, g, acols],
+                          h_codes[r * NG + g][:], h_scales[r * NG + g][:], g == 0, g == NG - 1)
+            u_bank[j] = bank
+
+        def u_tanh(j, lo, hi):
+            n, t = divmod(j, PACK)
+            tanh_u[j, lo] = work.tile([P, hi - lo], F32, tag="tanh_u", name="tanh_u", bufs=4)
+            nc.scalar.activation(out=tanh_u[j, lo][:], in_=u_bank[j][:, lo:hi], func=ACT.Tanh,
+                                 bias=column(ROW_BIAS + n % NG, t))
+
+        def y_affine(j, lo, hi):
+            n, t = divmod(j, PACK)
+            if t == 0 and lo == 0:
+                y_slots[n] = work.tile([P, PACK, F], F32, tag="y_slots", name="y_slots")
+            scale, offset = column(ROW_SCALE + n % NG, t), column(ROW_OFFSET + n, t)
+            if j < VECTOR_FREE_FROM and j % 2 == 1:
+                nc.scalar.activation(out=y_slots[n][:, t, lo:hi], in_=tanh_u[j, lo][:], func=ACT.Identity,
+                                     scale=scale, bias=offset)
+            else:
+                nc.vector.tensor_scalar(out=y_slots[n][:, t, lo:hi], in0=tanh_u[j, lo][:], scalar1=scale,
+                                        scalar2=offset, op0=ALU.mult, op1=ALU.add)
+
+        def y_interleave(n, lo, hi):
+            if lo == 0:
+                y_grouped[n] = work.tile([P, F, PACK], BF16, tag="y_grouped", name="y_grouped", align_bytes=64)
+            interleave(y_grouped[n][:, lo:hi, :], y_slots[n][:, :, lo:hi])
+
+        def y_quantize(n, lo, hi):
+            r, ag = divmod(n, NG)
+            if lo == 0:
+                y_codes[n] = work.tile([P, F], U32, tag="y_codes", name="y_codes", align_bytes=64)
+            quantize(y_codes[n][:, lo:hi], y_scales[PACK * ag:P, r * F + lo:r * F + hi],
+                     y_grouped[n][:, lo:hi, :].rearrange("p m t -> p (m t)"))
+
+        def words_store(n):
+            r, ag = divmod(n, NG)
+            nc.sync.dma_start(out=words_out[ag, :, r * F:(r + 1) * F], in_=y_codes[n][:].bitcast(I32))
+
+        def scales_store():
+            for q in range(4):
+                nc.sync.dma_start(out=scales_out[:, 4 * q:4 * q + 4, :],
+                                  in_=y_scales[32 * q:32 * q + NG * 4, :].bitcast(I32))
+
+        def y_transpose(l):
+            n, chunk = divmod(l, PACK)
+            y_bank[l] = turn_pool_bank([P, PACK, P])
+            for t in range(PACK):
+                nc.tensor.transpose(y_bank[l][:, t, :], y_slots[n][:, t, chunk * P:(chunk + 1) * P], ident[:])
+
+        def y_store(l):
+            n, chunk = divmod(l, PACK)
+            r, ag = divmod(n, NG)
+            width = 1 if l >= BANKS - 2 else 2
+            k = l % width
+            if k == 0:
+                y_rows[l] = work.tile([P, width, P, PACK], F32, tag="y_rows", name="y_rows", bufs=6)
+            rows = y_rows[l - k]
+            src = y_bank[l][:].rearrange("m t p -> m p t")
+            if (VECTOR_FREE_FROM <= l < LAST_GROUP and l % 2 == 0) or l == BANKS - 1:
+                nc.vector.tensor_copy(out=rows[:, k, :, :], in_=src)
+            else:
+                nc.scalar.copy(out=rows[:, k, :, :], in_=src)
+            if k == width - 1:
+                block = out_0[r, (chunk - k) * P:(chunk + 1) * P, ag * GROUP:(ag + 1) * GROUP]
+                nc.sync.dma_start(out=block.rearrange("(w m) a -> m w a", w=width),
+                                  in_=rows[:].rearrange("m w p t -> m w (p t)"))
+
+        def opening():
+            make_constants()
+            policy_interleave(0, 0)
+            policy_interleave(0, 1)
+            history_transpose(0, 0)
+            history_copy(0, 0)
+            history_transpose(0, 1)
+            policy_quantize(0)
+            encoder_interleave(0)
+            history_copy(0, 1)
+            history_quantize(0, 0, 1)
+            encoder_quantize(0)
+            history_quantize(0, 1, 2)
+            z_matmul(0)
+            encoder_interleave(1)
+            channel_rows()
+            encoder_quantize(1)
+            z_matmul(1)
+
+        def step(s):
+            j, l = s - STAGE2_LAG, s - TURN_LAG
+            hist_n, hist_h = divmod(s + 2, 2)
+            pol_n, pol_k = divmod(s + 5, PACK)
+            if 0 <= l < LAST_GROUP and l % 2 == 0:
+                y_transpose(l)
+                y_transpose(l + 1)
+            if hist_n < R * NG and hist_h == 0:
+                history_transpose(hist_n, 0)
+                history_transpose(hist_n, 1)
+            if 2 <= s + 1 < BANKS:
+                z_matmul(s + 1)
+            if 0 <= j < LAST_GROUP:
+                u_matmul(j)
+            if s < BANKS:
+                z_exp(s)
+            if 0 <= s - 1 < BANKS:
+                z_max(s - 1)
+            if 0 <= j - 2 < LAST_GROUP:
+                y_affine(j - 2, 0, F)
+            if 0 <= j - 1 < LAST_GROUP:
+                u_tanh(j - 1, 0, F)
+            if s % PACK == 2 and (s + 2) // PACK < R * NG:
+                history_quantize((s + 2) // PACK, 0, 2)
+            if s % PACK == 3 and NG <= (s + 1) // PACK < NG * NG:
+                policy_quantize((s + 1) // PACK)
+            if s % PACK == 1 and 0 <= s - 5 < BANKS:
+                h_quantize((s - 5) // PACK)
+            if (l + 1) % PACK == 0 and 0 <= l + 1 < LAST_GROUP:
+                y_interleave((l + 1) // PACK, 0, F)
+            if l % PACK == 0 and 0 <= l < LAST_GROUP:
+                y_quantize(l // PACK, 0, F)
+            if l % PACK == 1 and 0 <= l < LAST_GROUP:
+                words_store(l // PACK)
+            if hist_n < R * NG:
+                history_copy(hist_n, hist_h)
+            if NG <= pol_n < NG * NG and pol_k % 2 == 0:
+                policy_interleave(pol_n, pol_k // 2)
+            if 0 <= l < LAST_GROUP:
+                y_store(l)
+            if s % 2 == 0 and 2 <= s <= BANKS:
+                z_gain(s // 2 - 1)
+
+        def last_group(s):
+            n = LAST_GROUP // PACK
+            if s < 2:
+                u_matmul(LAST_GROUP + 2 * s)
+                u_matmul(LAST_GROUP + 2 * s + 1)
+            for lag, work_on in ((2, y_affine), (1, u_tanh)):
+                if 0 <= s - lag < PACK:
+                    h, pair = divmod(s - lag, 2)
+                    for t in (2 * pair, 2 * pair + 1):
+                        work_on(LAST_GROUP + t, h * HALF, (h + 1) * HALF)
+            for h in range(2):
+                if s == 5 + 2 * h:
+                    y_transpose(LAST_GROUP + 2 * h)
+                    y_transpose(LAST_GROUP + 2 * h + 1)
+                    y_interleave(n, h * HALF, (h + 1) * HALF)
+                    y_quantize(n, h * HALF, (h + 1) * HALF)
+                if s == 6 + 2 * h:
+                    y_store(LAST_GROUP + 2 * h)
+                    if h == 1:
+                        words_store(n)
+                    y_store(LAST_GROUP + 2 * h + 1)
+
+        with tc.manual_schedule(engines={ENGINE.SP}):
+            load_inputs()
+        opening()
+        policy_interleave(1, 0)
+        policy_interleave(1, 1)
+        channel_columns()
+        policy_quantize(1)
+        for s in range(PINNED_FROM):
+            step(s)
+        last_start = STAGE2_LAG + LAST_GROUP
+        with tc.manual_schedule(engines={ENGINE.SP, ENGINE.PE}):
+            for s in range(PINNED_FROM, last_start + 9):
+                step(s)
+                if s >= last_start:
+                    last_group(s - last_start)
+            scales_store()

@@ -14,22 +14,23 @@ U8 = mybir.dt.uint8
 FP8X4 = mybir.dt.float8_e4m3fn_x4
 ACT = mybir.ActivationFunctionType
 ALU = mybir.AluOpType
-ENGINE = mybir.EngineType
 
 P = 128
 PACK = 4
 GROUP = P * PACK
 NG = 2
 HALF = GROUP // 2
+Z_BANKS = 3
 BANKS = R * NG * PACK
 
 ROW_OFFSET, ROW_GAIN, ROW_BIAS, ROW_SCALE, ROWS = 0, 8, 10, 12, 14
 
 STAGE2_LAG = 10
 TURN_LAG = STAGE2_LAG + 6
-PINNED_FROM = 4
-VECTOR_FREE_FROM = 22
+AFFINE_ALL_VECTOR = 22
+COPY_SHARED = 20
 LAST_GROUP = BANKS - PACK
+STAGE1_OVER = 18
 
 
 def tile_legged_action_chunk_planes_h3_kernel(
@@ -39,16 +40,17 @@ def tile_legged_action_chunk_planes_h3_kernel(
     with ExitStack() as ctx:
         keep = ctx.enter_context(tc.tile_pool(name="keep", bufs=1))
         work = ctx.enter_context(tc.tile_pool(name="work", bufs=2))
-        psum = ctx.enter_context(tc.psum_pool(name="psum", bufs=1))
+        psum = ctx.enter_context(tc.psum_pool(name="psum", bufs=2))
+        ctx.enter_context(tc.manual_schedule())
 
-        def z_pool_bank(shape):
-            return psum.tile(shape, F32, tag="z", name="z", bufs=3)
+        def z_pool_bank(shape, name):
+            return psum.tile(shape, F32, tag="z", name=name, bufs=Z_BANKS)
 
-        def u_pool_bank(shape):
-            return psum.tile(shape, F32, tag="u", name="u", bufs=2)
+        def u_pool_bank(shape, name):
+            return psum.tile(shape, F32, tag="u", name=name, bufs=2)
 
-        def turn_pool_bank(shape):
-            return psum.tile(shape, F32, tag="turn", name="turn", bufs=3)
+        def turn_pool_bank(shape, name):
+            return psum.tile(shape, F32, tag="turn", name=name, bufs=3)
 
         def quantize(codes, scales, values):
             nc.vector.quantize_mx(out=codes.bitcast(FP8X4), scales=scales, in_=values)
@@ -66,59 +68,56 @@ def tile_legged_action_chunk_planes_h3_kernel(
             return history[r, g * GROUP:(g + 1) * GROUP, :].rearrange("(m t) k -> m t k", t=PACK)
 
         def load_history(n):
-            raw = keep.tile([P, PACK, T], BF16, name="hist_%d" % n)
+            raw = keep.tile([P, PACK, T], BF16, name="hist_%d_%d" % divmod(n, NG))
             nc.sync.dma_start(out=raw[:], in_=history_rows(n))
             for h in range(2):
                 hist_raw[n, h] = raw[:, 2 * h:2 * h + 2, :]
 
         def load_policy(n):
             ag, g = divmod(n, NG)
-            pol_raw[n] = keep.tile([P, PACK, GROUP], BF16, name="pol_%d" % n)
+            pol_raw[n] = keep.tile([P, PACK, GROUP], BF16, name="pol_%d_%d" % (g, ag))
             block = policy[g * GROUP:(g + 1) * GROUP, ag * GROUP:(ag + 1) * GROUP]
             nc.sync.dma_start(out=pol_raw[n][:], in_=block.rearrange("(p j) a -> p j a", j=PACK))
 
-        def load_inputs():
-            load_policy(0)
-            for h in range(2):
-                raw = keep.tile([P, 2, T], BF16, name="hist_0_%d" % h)
-                nc.sync.dma_start(out=raw[:], in_=history_rows(0)[:, 2 * h:2 * h + 2, :])
-                hist_raw[0, h] = raw[:]
-            nc.sync.dma_start(out=enc_raw[:], in_=encoder.rearrange("(p j) f -> p j f", j=PACK))
-            nc.sync.dma_start(out=rows_bf[ROW_OFFSET:ROW_OFFSET + R * NG, :],
-                              in_=pose_offset.rearrange("r (g c) -> (r g) c", g=NG))
-            for row, vec in ((ROW_GAIN, sensor_gain), (ROW_BIAS, policy_bias), (ROW_SCALE, action_scale)):
-                nc.sync.dma_start(out=rows_bf[row:row + NG, :], in_=vec.rearrange("(g c) -> g c", g=NG))
-            for n in range(1, R * NG):
-                if n < NG * NG:
-                    load_policy(n)
-                load_history(n)
+        load_policy(0)
+        for h in range(2):
+            raw = keep.tile([P, 2, T], BF16, name="hist_0_0_%d" % h)
+            nc.sync.dma_start(out=raw[:], in_=history_rows(0)[:, 2 * h:2 * h + 2, :])
+            hist_raw[0, h] = raw[:]
+        nc.sync.dma_start(out=enc_raw[:], in_=encoder.rearrange("(p j) f -> p j f", j=PACK))
+        nc.sync.dma_start(out=rows_bf[ROW_OFFSET:ROW_OFFSET + R * NG, :],
+                          in_=pose_offset.rearrange("r (g c) -> (r g) c", g=NG))
+        for row, vec in ((ROW_GAIN, sensor_gain), (ROW_BIAS, policy_bias), (ROW_SCALE, action_scale)):
+            nc.sync.dma_start(out=rows_bf[row:row + NG, :], in_=vec.rearrange("(g c) -> g c", g=NG))
+        load_policy(1)
+        load_history(1)
+        for n in range(2, R * NG):
+            load_history(n)
+            if n < NG * NG:
+                load_policy(n)
 
         ident = keep.tile([P, P], F32)
+        make_identity(nc, ident[:])
         rows_f = keep.tile([P, GROUP], F32)
-        table_load = keep.tile([P, 1], F32)
+        nc.vector.memset(rows_f[:], 0.0)
         chan = keep.tile([P, ROWS, PACK], F32)
         one_values = keep.tile([P, P * PACK], BF16, align_bytes=64)
+        nc.vector.memset(one_values[:], 1.0)
+        frac_values = keep.tile([P, GROUP * PACK], BF16, align_bytes=64)
+        nc.vector.memset(frac_values[:], 1.0 / GROUP)
         one_codes = keep.tile([P, P], U32, align_bytes=64)
         one_scales = keep.tile([P, P], U8, align_bytes=64)
-        frac_values = keep.tile([P, GROUP * PACK], BF16, align_bytes=64)
         frac_codes = keep.tile([P, GROUP], U32, align_bytes=64)
         frac_scales = keep.tile([P, GROUP], U8, align_bytes=64)
-
-        def make_constants():
-            make_identity(nc, ident[:])
-            nc.vector.memset(rows_f[:], 0.0)
-            nc.scalar.activation(out=table_load[:], in_=rows_f[:, 0:1], func=ACT.Exp)
-            nc.vector.memset(one_values[:], 1.0)
-            nc.vector.memset(frac_values[:], 1.0 / GROUP)
-            quantize(one_codes[:], one_scales[:], one_values[:])
-            quantize(frac_codes[:], frac_scales[:], frac_values[:])
+        quantize(one_codes[:], one_scales[:], one_values[:])
+        quantize(frac_codes[:], frac_scales[:], frac_values[:])
 
         def channel_rows():
-            nc.scalar.copy(out=rows_f[0:ROWS, :].rearrange("q (t p) -> q t p", t=PACK),
-                           in_=rows_bf[0:ROWS, :].rearrange("q (p t) -> q t p", t=PACK))
+            nc.scalar.copy(out=rows_f[0:ROWS, :].rearrange("row (t p) -> row t p", t=PACK),
+                           in_=rows_bf[0:ROWS, :].rearrange("row (p t) -> row t p", t=PACK))
 
         def channel_columns():
-            bank = u_pool_bank([P, P, PACK])
+            bank = u_pool_bank([P, P, PACK], "chan_ps")
             for t in range(PACK):
                 nc.tensor.transpose(bank[:, :, t], rows_f[:, t * P:(t + 1) * P], ident[:])
             nc.scalar.copy(out=chan[:], in_=bank[:, 0:ROWS, :])
@@ -145,7 +144,7 @@ def tile_legged_action_chunk_planes_h3_kernel(
         hist_bank, hist_grouped, hist_codes, hist_scales = {}, {}, {}, {}
 
         def history_transpose(n, h):
-            bank = turn_pool_bank([P, 2, 2, P])
+            bank = turn_pool_bank([P, 2, 2, P], "bank")
             for t in range(2):
                 words = hist_raw[n, h][:, t, :].bitcast(F32)
                 for u in range(2):
@@ -161,8 +160,8 @@ def tile_legged_action_chunk_planes_h3_kernel(
 
         def history_quantize(n, first, last):
             if first == 0:
-                hist_codes[n] = keep.tile([P, GROUP], U32, name="hist_codes_%d" % n, align_bytes=64)
-                hist_scales[n] = keep.tile([P, GROUP], U8, name="hist_scales_%d" % n, align_bytes=64)
+                hist_codes[n] = keep.tile([P, GROUP], U32, name="hist_codes_%d_%d" % divmod(n, NG), align_bytes=64)
+                hist_scales[n] = keep.tile([P, GROUP], U8, name="hist_scales_%d_%d" % divmod(n, NG), align_bytes=64)
             cols = slice(first * HALF, last * HALF)
             quantize(hist_codes[n][:, cols], hist_scales[n][:, cols],
                      hist_grouped[n][:, first:last, :].rearrange("p h c -> p (h c)"))
@@ -177,7 +176,7 @@ def tile_legged_action_chunk_planes_h3_kernel(
                                            align_bytes=64)
             dst = pol_grouped[n][:, 2 * h:2 * h + 2, :, :]
             src = pol_raw[n][:].rearrange("p j (m t) -> p t m j", t=PACK)[:, 2 * h:2 * h + 2, :, :]
-            if h == 1 and n < NG:
+            if h == 1 and n < NG * NG - 1:
                 nc.vector.tensor_copy(out=dst, in_=src)
             else:
                 nc.scalar.copy(out=dst, in_=src)
@@ -191,7 +190,7 @@ def tile_legged_action_chunk_planes_h3_kernel(
 
         def z_matmul(i):
             n, chunk = divmod(i, PACK)
-            bank = z_pool_bank([P, PACK, P])
+            bank = z_pool_bank([P, PACK, P], "bank")
             mx_matmul(bank[:].rearrange("p t f -> p (t f)"), one_codes[:], one_scales[:], frac_codes[:], frac_scales[:],
                       True, False)
             fcols = slice(chunk * P, (chunk + 1) * P)
@@ -202,13 +201,13 @@ def tile_legged_action_chunk_planes_h3_kernel(
             z_bank[i] = bank[:].rearrange("p t f -> p f t")
 
         def z_exp(i):
-            exp_z[i] = work.tile([P, P, PACK], F32, tag="exp_z", name="exp_z", bufs=3)
+            exp_z[i] = work.tile([P, P, PACK], F32, tag="e", name="e", bufs=Z_BANKS)
             nc.scalar.activation(out=exp_z[i][:], in_=z_bank[i], func=ACT.Exp, bias=-1.0)
 
         def z_max(i):
             pair, k = divmod(i, 2)
             if k == 0:
-                elu_one[pair] = work.tile([P, 2 * P, PACK], F32, tag="elu_one", name="elu_one")
+                elu_one[pair] = work.tile([P, 2 * P, PACK], F32, tag="m", name="m")
             nc.vector.scalar_tensor_tensor(out=elu_one[pair][:, k * P:(k + 1) * P, :], in0=exp_z[i][:], scalar=1.0,
                                            in1=z_bank[i], op0=ALU.min, op1=ALU.max)
 
@@ -234,30 +233,29 @@ def tile_legged_action_chunk_planes_h3_kernel(
         def u_matmul(j):
             n, t = divmod(j, PACK)
             r, ag = divmod(n, NG)
-            bank = z_pool_bank([P, F]) if j > LAST_GROUP else u_pool_bank([P, F])
+            bank = u_pool_bank([P, F], "bank")
             acols = slice(ag * GROUP + t * P, ag * GROUP + (t + 1) * P)
             for g in range(NG):
                 mx_matmul(bank[:], pol_codes[:, g, acols], pol_scales[:, g, acols],
                           h_codes[r * NG + g][:], h_scales[r * NG + g][:], g == 0, g == NG - 1)
             u_bank[j] = bank
 
-        def u_tanh(j, lo, hi):
+        def u_tanh(j):
             n, t = divmod(j, PACK)
-            tanh_u[j, lo] = work.tile([P, hi - lo], F32, tag="tanh_u", name="tanh_u", bufs=4)
-            nc.scalar.activation(out=tanh_u[j, lo][:], in_=u_bank[j][:, lo:hi], func=ACT.Tanh,
-                                 bias=column(ROW_BIAS + n % NG, t))
+            tanh_u[j] = work.tile([P, F], F32, tag="th", name="th", bufs=3)
+            nc.scalar.activation(out=tanh_u[j][:], in_=u_bank[j][:], func=ACT.Tanh, bias=column(ROW_BIAS + n % NG, t))
 
-        def y_affine(j, lo, hi):
+        def y_affine(j):
             n, t = divmod(j, PACK)
-            if t == 0 and lo == 0:
-                y_slots[n] = work.tile([P, PACK, F], F32, tag="y_slots", name="y_slots")
+            if t == 0:
+                y_slots[n] = work.tile([P, PACK, F], F32, tag="y", name="y")
             scale, offset = column(ROW_SCALE + n % NG, t), column(ROW_OFFSET + n, t)
-            if j < VECTOR_FREE_FROM and j % 2 == 1:
-                nc.scalar.activation(out=y_slots[n][:, t, lo:hi], in_=tanh_u[j, lo][:], func=ACT.Identity,
+            if j < AFFINE_ALL_VECTOR and j % 2 == 1:
+                nc.scalar.activation(out=y_slots[n][:, t, :], in_=tanh_u[j][:], func=ACT.Identity,
                                      scale=scale, bias=offset)
             else:
-                nc.vector.tensor_scalar(out=y_slots[n][:, t, lo:hi], in0=tanh_u[j, lo][:], scalar1=scale,
-                                        scalar2=offset, op0=ALU.mult, op1=ALU.add)
+                nc.vector.tensor_scalar(out=y_slots[n][:, t, :], in0=tanh_u[j][:], scalar1=scale, scalar2=offset,
+                                        op0=ALU.mult, op1=ALU.add)
 
         def y_interleave(n, lo, hi):
             if lo == 0:
@@ -280,22 +278,26 @@ def tile_legged_action_chunk_planes_h3_kernel(
                 nc.sync.dma_start(out=scales_out[:, 4 * q:4 * q + 4, :],
                                   in_=y_scales[32 * q:32 * q + NG * 4, :].bitcast(I32))
 
-        def y_transpose(l):
+        def y_transpose(l, slots):
             n, chunk = divmod(l, PACK)
-            y_bank[l] = turn_pool_bank([P, PACK, P])
-            for t in range(PACK):
+            if slots[0] == 0:
+                if (STAGE1_OVER <= l < STAGE1_OVER + 2 * Z_BANKS and l % 2 == 1) or l > LAST_GROUP:
+                    y_bank[l] = z_pool_bank([P, PACK, P], "z")
+                else:
+                    y_bank[l] = turn_pool_bank([P, PACK, P], "turn")
+            for t in slots:
                 nc.tensor.transpose(y_bank[l][:, t, :], y_slots[n][:, t, chunk * P:(chunk + 1) * P], ident[:])
 
         def y_store(l):
             n, chunk = divmod(l, PACK)
             r, ag = divmod(n, NG)
-            width = 1 if l >= BANKS - 2 else 2
+            width = 1 if l >= LAST_GROUP else 2
             k = l % width
             if k == 0:
                 y_rows[l] = work.tile([P, width, P, PACK], F32, tag="y_rows", name="y_rows", bufs=6)
             rows = y_rows[l - k]
             src = y_bank[l][:].rearrange("m t p -> m p t")
-            if (VECTOR_FREE_FROM <= l < LAST_GROUP and l % 2 == 0) or l == BANKS - 1:
+            if COPY_SHARED <= l < LAST_GROUP and l % 2 == 0:
                 nc.vector.tensor_copy(out=rows[:, k, :, :], in_=src)
             else:
                 nc.scalar.copy(out=rows[:, k, :, :], in_=src)
@@ -305,48 +307,58 @@ def tile_legged_action_chunk_planes_h3_kernel(
                                   in_=rows[:].rearrange("m w p t -> m w (p t)"))
 
         def opening():
-            make_constants()
             policy_interleave(0, 0)
             policy_interleave(0, 1)
+            policy_quantize(0)
+            encoder_interleave(0)
+            encoder_interleave(1)
             history_transpose(0, 0)
             history_copy(0, 0)
             history_transpose(0, 1)
-            policy_quantize(0)
-            encoder_interleave(0)
-            history_copy(0, 1)
             history_quantize(0, 0, 1)
             encoder_quantize(0)
+            history_copy(0, 1)
             history_quantize(0, 1, 2)
-            z_matmul(0)
-            encoder_interleave(1)
-            channel_rows()
             encoder_quantize(1)
+            z_matmul(0)
+            channel_rows()
+            policy_interleave(1, 0)
+            policy_interleave(1, 1)
             z_matmul(1)
+            policy_quantize(1)
+            z_exp(0)
+            channel_columns()
 
         def step(s):
             j, l = s - STAGE2_LAG, s - TURN_LAG
             hist_n, hist_h = divmod(s + 2, 2)
             pol_n, pol_k = divmod(s + 5, PACK)
             if 0 <= l < LAST_GROUP and l % 2 == 0:
-                y_transpose(l)
-                y_transpose(l + 1)
+                y_transpose(l, range(PACK))
+                y_transpose(l + 1, range(PACK))
             if hist_n < R * NG and hist_h == 0:
                 history_transpose(hist_n, 0)
                 history_transpose(hist_n, 1)
             if 2 <= s + 1 < BANKS:
                 z_matmul(s + 1)
-            if 0 <= j < LAST_GROUP:
+            if 0 <= j < BANKS:
                 u_matmul(j)
-            if s < BANKS:
+            if 1 <= s < BANKS:
                 z_exp(s)
             if 0 <= s - 1 < BANKS:
                 z_max(s - 1)
-            if 0 <= j - 2 < LAST_GROUP:
-                y_affine(j - 2, 0, F)
-            if 0 <= j - 1 < LAST_GROUP:
-                u_tanh(j - 1, 0, F)
+            if j - 2 == BANKS - 1:
+                turn_last_group((2,))
+            if 0 <= j - 2 < BANKS:
+                y_affine(j - 2)
+            if 0 <= j - 1 < BANKS:
+                u_tanh(j - 1)
+            if j - 2 == BANKS - 1:
+                finish_last_group()
             if s % PACK == 2 and (s + 2) // PACK < R * NG:
                 history_quantize((s + 2) // PACK, 0, 2)
+            if pol_n == NG and pol_k == 2:
+                policy_interleave(pol_n, 1)
             if s % PACK == 3 and NG <= (s + 1) // PACK < NG * NG:
                 policy_quantize((s + 1) // PACK)
             if s % PACK == 1 and 0 <= s - 5 < BANKS:
@@ -357,50 +369,30 @@ def tile_legged_action_chunk_planes_h3_kernel(
                 y_quantize(l // PACK, 0, F)
             if l % PACK == 1 and 0 <= l < LAST_GROUP:
                 words_store(l // PACK)
+            if l == BANKS - 2:
+                words_store(LAST_GROUP // PACK)
+                scales_store()
             if hist_n < R * NG:
                 history_copy(hist_n, hist_h)
-            if NG <= pol_n < NG * NG and pol_k % 2 == 0:
+            if (NG <= pol_n < NG * NG and pol_k == 0) or (pol_n == NG * NG - 1 and pol_k == 2):
                 policy_interleave(pol_n, pol_k // 2)
-            if 0 <= l < LAST_GROUP:
+            if j - 2 == BANKS - 2:
+                turn_last_group((0, 1))
+            if 0 <= l < BANKS:
                 y_store(l)
             if s % 2 == 0 and 2 <= s <= BANKS:
                 z_gain(s // 2 - 1)
 
-        def last_group(s):
-            n = LAST_GROUP // PACK
-            if s < 2:
-                u_matmul(LAST_GROUP + 2 * s)
-                u_matmul(LAST_GROUP + 2 * s + 1)
-            for lag, work_on in ((2, y_affine), (1, u_tanh)):
-                if 0 <= s - lag < PACK:
-                    h, pair = divmod(s - lag, 2)
-                    for t in (2 * pair, 2 * pair + 1):
-                        work_on(LAST_GROUP + t, h * HALF, (h + 1) * HALF)
-            for h in range(2):
-                if s == 5 + 2 * h:
-                    y_transpose(LAST_GROUP + 2 * h)
-                    y_transpose(LAST_GROUP + 2 * h + 1)
-                    y_interleave(n, h * HALF, (h + 1) * HALF)
-                    y_quantize(n, h * HALF, (h + 1) * HALF)
-                if s == 6 + 2 * h:
-                    y_store(LAST_GROUP + 2 * h)
-                    if h == 1:
-                        words_store(n)
-                    y_store(LAST_GROUP + 2 * h + 1)
+        def turn_last_group(slots):
+            for l in range(LAST_GROUP, BANKS):
+                y_transpose(l, slots)
 
-        with tc.manual_schedule(engines={ENGINE.SP}):
-            load_inputs()
+        def finish_last_group():
+            turn_last_group((3,))
+            for work_on in (y_interleave, y_quantize):
+                for h in range(2):
+                    work_on(LAST_GROUP // PACK, h * HALF, (h + 1) * HALF)
+
         opening()
-        policy_interleave(1, 0)
-        policy_interleave(1, 1)
-        channel_columns()
-        policy_quantize(1)
-        for s in range(PINNED_FROM):
+        for s in range(TURN_LAG + BANKS):
             step(s)
-        last_start = STAGE2_LAG + LAST_GROUP
-        with tc.manual_schedule(engines={ENGINE.SP, ENGINE.PE}):
-            for s in range(PINNED_FROM, last_start + 9):
-                step(s)
-                if s >= last_start:
-                    last_group(s - last_start)
-            scales_store()

from contextlib import ExitStack

import concourse.mybir as mybir
from concourse.masks import make_identity

R, S, T, F, A = 4, 1024, 512, 512, 1024
FLOPS = 2 * R * S * T * F + 2 * R * F * S * A

F32 = mybir.dt.float32
BF16 = mybir.dt.bfloat16
U32 = mybir.dt.uint32
I32 = mybir.dt.int32
U8 = mybir.dt.uint8
FP8X4 = mybir.dt.float8_e4m3fn_x4
ACT = mybir.ActivationFunctionType
ALU = mybir.AluOpType

P = 128
PACK = 4
GROUP = P * PACK
NG = 2
HALF = GROUP // 2
Z_BANKS = 3
BANKS = R * NG * PACK

ROW_OFFSET, ROW_GAIN, ROW_BIAS, ROW_SCALE, ROWS = 0, 8, 10, 12, 14

STAGE2_LAG = 10
TURN_LAG = STAGE2_LAG + 6
AFFINE_ALL_VECTOR = 22
COPY_SHARED = 20
LAST_GROUP = BANKS - PACK
STAGE1_OVER = 18


def tile_legged_action_chunk_planes_h3_kernel(
    tc, history, encoder, sensor_gain, policy, policy_bias, action_scale, pose_offset, out_0, out_1, out_2
):
    nc = tc.nc
    with ExitStack() as ctx:
        keep = ctx.enter_context(tc.tile_pool(name="keep", bufs=1))
        work = ctx.enter_context(tc.tile_pool(name="work", bufs=2))
        psum = ctx.enter_context(tc.psum_pool(name="psum", bufs=2))
        ctx.enter_context(tc.manual_schedule())

        def z_pool_bank(shape, name):
            return psum.tile(shape, F32, tag="z", name=name, bufs=Z_BANKS)

        def u_pool_bank(shape, name):
            return psum.tile(shape, F32, tag="u", name=name, bufs=2)

        def turn_pool_bank(shape, name):
            return psum.tile(shape, F32, tag="turn", name=name, bufs=3)

        def quantize(codes, scales, values):
            nc.vector.quantize_mx(out=codes.bitcast(FP8X4), scales=scales, in_=values)

        def mx_matmul(out, lhs_codes, lhs_scales, rhs_codes, rhs_scales, start, stop):
            nc.tensor.matmul_mx(out=out, lhsT=lhs_codes.bitcast(FP8X4), lhsT_scale=lhs_scales,
                                rhs=rhs_codes.bitcast(FP8X4), rhs_scale=rhs_scales, start=start, stop=stop)

        hist_raw, pol_raw = {}, {}
        enc_raw = keep.tile([P, PACK, F], BF16)
        rows_bf = keep.tile([P, GROUP], BF16)

        def history_rows(n):
            r, g = divmod(n, NG)
            return history[r, g * GROUP:(g + 1) * GROUP, :].rearrange("(m t) k -> m t k", t=PACK)

        def load_history(n):
            raw = keep.tile([P, PACK, T], BF16, name="hist_%d_%d" % divmod(n, NG))
            nc.sync.dma_start(out=raw[:], in_=history_rows(n))
            for h in range(2):
                hist_raw[n, h] = raw[:, 2 * h:2 * h + 2, :]

        def load_policy(n):
            ag, g = divmod(n, NG)
            pol_raw[n] = keep.tile([P, PACK, GROUP], BF16, name="pol_%d_%d" % (g, ag))
            block = policy[g * GROUP:(g + 1) * GROUP, ag * GROUP:(ag + 1) * GROUP]
            nc.sync.dma_start(out=pol_raw[n][:], in_=block.rearrange("(p j) a -> p j a", j=PACK))

        load_policy(0)
        for h in range(2):
            raw = keep.tile([P, 2, T], BF16, name="hist_0_0_%d" % h)
            nc.sync.dma_start(out=raw[:], in_=history_rows(0)[:, 2 * h:2 * h + 2, :])
            hist_raw[0, h] = raw[:]
        nc.sync.dma_start(out=enc_raw[:], in_=encoder.rearrange("(p j) f -> p j f", j=PACK))
        nc.sync.dma_start(out=rows_bf[ROW_OFFSET:ROW_OFFSET + R * NG, :],
                          in_=pose_offset.rearrange("r (g c) -> (r g) c", g=NG))
        for row, vec in ((ROW_GAIN, sensor_gain), (ROW_BIAS, policy_bias), (ROW_SCALE, action_scale)):
            nc.sync.dma_start(out=rows_bf[row:row + NG, :], in_=vec.rearrange("(g c) -> g c", g=NG))
        load_policy(1)
        load_history(1)
        for n in range(2, R * NG):
            load_history(n)
            if n < NG * NG:
                load_policy(n)

        ident = keep.tile([P, P], F32)
        make_identity(nc, ident[:])
        rows_f = keep.tile([P, GROUP], F32)
        nc.vector.memset(rows_f[:], 0.0)
        chan = keep.tile([P, ROWS, PACK], F32)
        one_values = keep.tile([P, P * PACK], BF16, align_bytes=64)
        nc.vector.memset(one_values[:], 1.0)
        frac_values = keep.tile([P, GROUP * PACK], BF16, align_bytes=64)
        nc.vector.memset(frac_values[:], 1.0 / GROUP)
        one_codes = keep.tile([P, P], U32, align_bytes=64)
        one_scales = keep.tile([P, P], U8, align_bytes=64)
        frac_codes = keep.tile([P, GROUP], U32, align_bytes=64)
        frac_scales = keep.tile([P, GROUP], U8, align_bytes=64)
        quantize(one_codes[:], one_scales[:], one_values[:])
        quantize(frac_codes[:], frac_scales[:], frac_values[:])

        def channel_rows():
            nc.scalar.copy(out=rows_f[0:ROWS, :].rearrange("row (t p) -> row t p", t=PACK),
                           in_=rows_bf[0:ROWS, :].rearrange("row (p t) -> row t p", t=PACK))

        def channel_columns():
            bank = u_pool_bank([P, P, PACK], "chan_ps")
            for t in range(PACK):
                nc.tensor.transpose(bank[:, :, t], rows_f[:, t * P:(t + 1) * P], ident[:])
            nc.scalar.copy(out=chan[:], in_=bank[:, 0:ROWS, :])

        def column(row, t):
            return chan[:, row, t:t + 1]

        enc_grouped = keep.tile([P, F, PACK], BF16, align_bytes=64)
        enc_codes = keep.tile([P, F], U32, align_bytes=64)
        enc_scales = keep.tile([P, F], U8, align_bytes=64)

        def interleave(dst, src):
            nc.vector.tensor_copy(out=dst.rearrange("p (c i) t -> p c t i", i=4),
                                  in_=src.rearrange("p t (c i) -> p c t i", i=4))

        def encoder_interleave(h):
            cols = slice(h * HALF, (h + 1) * HALF)
            interleave(enc_grouped[:, cols, :], enc_raw[:, :, cols])

        def encoder_quantize(h):
            cols = slice(h * HALF, (h + 1) * HALF)
            quantize(enc_codes[:, cols], enc_scales[:, cols], enc_grouped[:, cols, :].rearrange("p f j -> p (f j)"))

        hist_bank, hist_grouped, hist_codes, hist_scales = {}, {}, {}, {}

        def history_transpose(n, h):
            bank = turn_pool_bank([P, 2, 2, P], "bank")
            for t in range(2):
                words = hist_raw[n, h][:, t, :].bitcast(F32)
                for u in range(2):
                    nc.tensor.transpose(bank[:, t, u, :], words[:, u:T // 2:2], ident[:])
            hist_bank[n, h] = bank

        def history_copy(n, h):
            if h == 0:
                hist_grouped[n] = work.tile([P, 2, 2 * P * PACK], BF16, tag="hist_grouped", name="hist_grouped",
                                            bufs=5, align_bytes=64)
            nc.scalar.copy(out=hist_grouped[n][:, h, :].bitcast(F32).rearrange("p (t m u) -> p t m u", t=2, u=2),
                           in_=hist_bank[n, h][:].rearrange("p t u m -> p t m u"))

        def history_quantize(n, first, last):
            if first == 0:
                hist_codes[n] = keep.tile([P, GROUP], U32, name="hist_codes_%d_%d" % divmod(n, NG), align_bytes=64)
                hist_scales[n] = keep.tile([P, GROUP], U8, name="hist_scales_%d_%d" % divmod(n, NG), align_bytes=64)
            cols = slice(first * HALF, last * HALF)
            quantize(hist_codes[n][:, cols], hist_scales[n][:, cols],
                     hist_grouped[n][:, first:last, :].rearrange("p h c -> p (h c)"))

        pol_codes = keep.tile([P, NG, A], U32, align_bytes=64)
        pol_scales = keep.tile([P, NG, A], U8, align_bytes=64)
        pol_grouped = {}

        def policy_interleave(n, h):
            if h == 0:
                pol_grouped[n] = work.tile([P, PACK, P, PACK], BF16, tag="pol_grouped", name="pol_grouped",
                                           align_bytes=64)
            dst = pol_grouped[n][:, 2 * h:2 * h + 2, :, :]
            src = pol_raw[n][:].rearrange("p j (m t) -> p t m j", t=PACK)[:, 2 * h:2 * h + 2, :, :]
            if h == 1 and n < NG * NG - 1:
                nc.vector.tensor_copy(out=dst, in_=src)
            else:
                nc.scalar.copy(out=dst, in_=src)

        def policy_quantize(n):
            ag, g = divmod(n, NG)
            cols = slice(ag * GROUP, (ag + 1) * GROUP)
            quantize(pol_codes[:, g, cols], pol_scales[:, g, cols], pol_grouped[n][:].rearrange("p t m j -> p (t m j)"))

        z_bank, exp_z, elu_one, h_grouped, h_codes, h_scales = {}, {}, {}, {}, {}, {}

        def z_matmul(i):
            n, chunk = divmod(i, PACK)
            bank = z_pool_bank([P, PACK, P], "bank")
            mx_matmul(bank[:].rearrange("p t f -> p (t f)"), one_codes[:], one_scales[:], frac_codes[:], frac_scales[:],
                      True, False)
            fcols = slice(chunk * P, (chunk + 1) * P)
            for t in range(PACK):
                scols = slice(t * P, (t + 1) * P)
                mx_matmul(bank[:, t, :], hist_codes[n][:, scols], hist_scales[n][:, scols],
                          enc_codes[:, fcols], enc_scales[:, fcols], False, t == PACK - 1)
            z_bank[i] = bank[:].rearrange("p t f -> p f t")

        def z_exp(i):
            exp_z[i] = work.tile([P, P, PACK], F32, tag="e", name="e", bufs=Z_BANKS)
            nc.scalar.activation(out=exp_z[i][:], in_=z_bank[i], func=ACT.Exp, bias=-1.0)

        def z_max(i):
            pair, k = divmod(i, 2)
            if k == 0:
                elu_one[pair] = work.tile([P, 2 * P, PACK], F32, tag="m", name="m")
            nc.vector.scalar_tensor_tensor(out=elu_one[pair][:, k * P:(k + 1) * P, :], in0=exp_z[i][:], scalar=1.0,
                                           in1=z_bank[i], op0=ALU.min, op1=ALU.max)

        def z_gain(pair):
            n, h = divmod(pair, 2)
            if h == 0:
                h_grouped[n] = work.tile([P, F, PACK], BF16, tag="h_grouped", name="h_grouped", align_bytes=64)
            row = ROW_GAIN + n % NG
            nc.vector.scalar_tensor_tensor(out=h_grouped[n][:, h * HALF:(h + 1) * HALF, :], in0=elu_one[pair][:],
                                           scalar=-1.0, in1=chan[:, row:row + 1, :].to_broadcast([P, HALF, PACK]),
                                           op0=ALU.add, op1=ALU.mult)

        def h_quantize(n):
            h_codes[n] = work.tile([P, F], U32, tag="h_codes", name="h_codes", bufs=4, align_bytes=64)
            h_scales[n] = work.tile([P, F], U8, tag="h_scales", name="h_scales", bufs=4, align_bytes=64)
            quantize(h_codes[n][:], h_scales[n][:], h_grouped[n][:].rearrange("p f t -> p (f t)"))

        u_bank, tanh_u, y_slots, y_grouped, y_codes, y_bank, y_rows = {}, {}, {}, {}, {}, {}, {}
        y_scales = keep.tile([P, R * F], U8, align_bytes=64)
        words_out = out_1.rearrange("g p m t -> g p (m t)").bitcast(I32)
        scales_out = out_2.bitcast(I32)

        def u_matmul(j):
            n, t = divmod(j, PACK)
            r, ag = divmod(n, NG)
            bank = u_pool_bank([P, F], "bank")
            acols = slice(ag * GROUP + t * P, ag * GROUP + (t + 1) * P)
            for g in range(NG):
                mx_matmul(bank[:], pol_codes[:, g, acols], pol_scales[:, g, acols],
                          h_codes[r * NG + g][:], h_scales[r * NG + g][:], g == 0, g == NG - 1)
            u_bank[j] = bank

        def u_tanh(j):
            n, t = divmod(j, PACK)
            tanh_u[j] = work.tile([P, F], F32, tag="th", name="th", bufs=3)
            nc.scalar.activation(out=tanh_u[j][:], in_=u_bank[j][:], func=ACT.Tanh, bias=column(ROW_BIAS + n % NG, t))

        def y_affine(j):
            n, t = divmod(j, PACK)
            if t == 0:
                y_slots[n] = work.tile([P, PACK, F], F32, tag="y", name="y")
            scale, offset = column(ROW_SCALE + n % NG, t), column(ROW_OFFSET + n, t)
            if j < AFFINE_ALL_VECTOR and j % 2 == 1:
                nc.scalar.activation(out=y_slots[n][:, t, :], in_=tanh_u[j][:], func=ACT.Identity,
                                     scale=scale, bias=offset)
            else:
                nc.vector.tensor_scalar(out=y_slots[n][:, t, :], in0=tanh_u[j][:], scalar1=scale, scalar2=offset,
                                        op0=ALU.mult, op1=ALU.add)

        def y_interleave(n, lo, hi):
            if lo == 0:
                y_grouped[n] = work.tile([P, F, PACK], BF16, tag="y_grouped", name="y_grouped", align_bytes=64)
            interleave(y_grouped[n][:, lo:hi, :], y_slots[n][:, :, lo:hi])

        def y_quantize(n, lo, hi):
            r, ag = divmod(n, NG)
            if lo == 0:
                y_codes[n] = work.tile([P, F], U32, tag="y_codes", name="y_codes", align_bytes=64)
            quantize(y_codes[n][:, lo:hi], y_scales[PACK * ag:P, r * F + lo:r * F + hi],
                     y_grouped[n][:, lo:hi, :].rearrange("p m t -> p (m t)"))

        def words_store(n):
            r, ag = divmod(n, NG)
            nc.sync.dma_start(out=words_out[ag, :, r * F:(r + 1) * F], in_=y_codes[n][:].bitcast(I32))

        def scales_store():
            for q in range(4):
                nc.sync.dma_start(out=scales_out[:, 4 * q:4 * q + 4, :],
                                  in_=y_scales[32 * q:32 * q + NG * 4, :].bitcast(I32))

        def y_transpose(l, slots):
            n, chunk = divmod(l, PACK)
            if slots[0] == 0:
                if (STAGE1_OVER <= l < STAGE1_OVER + 2 * Z_BANKS and l % 2 == 1) or l > LAST_GROUP:
                    y_bank[l] = z_pool_bank([P, PACK, P], "z")
                else:
                    y_bank[l] = turn_pool_bank([P, PACK, P], "turn")
            for t in slots:
                nc.tensor.transpose(y_bank[l][:, t, :], y_slots[n][:, t, chunk * P:(chunk + 1) * P], ident[:])

        def y_store(l):
            n, chunk = divmod(l, PACK)
            r, ag = divmod(n, NG)
            width = 1 if l >= LAST_GROUP else 2
            k = l % width
            if k == 0:
                y_rows[l] = work.tile([P, width, P, PACK], F32, tag="y_rows", name="y_rows", bufs=6)
            rows = y_rows[l - k]
            src = y_bank[l][:].rearrange("m t p -> m p t")
            if COPY_SHARED <= l < LAST_GROUP and l % 2 == 0:
                nc.vector.tensor_copy(out=rows[:, k, :, :], in_=src)
            else:
                nc.scalar.copy(out=rows[:, k, :, :], in_=src)
            if k == width - 1:
                block = out_0[r, (chunk - k) * P:(chunk + 1) * P, ag * GROUP:(ag + 1) * GROUP]
                nc.sync.dma_start(out=block.rearrange("(w m) a -> m w a", w=width),
                                  in_=rows[:].rearrange("m w p t -> m w (p t)"))

        def opening():
            policy_interleave(0, 0)
            policy_interleave(0, 1)
            policy_quantize(0)
            encoder_interleave(0)
            encoder_interleave(1)
            history_transpose(0, 0)
            history_copy(0, 0)
            history_transpose(0, 1)
            history_quantize(0, 0, 1)
            encoder_quantize(0)
            history_copy(0, 1)
            history_quantize(0, 1, 2)
            encoder_quantize(1)
            z_matmul(0)
            channel_rows()
            policy_interleave(1, 0)
            policy_interleave(1, 1)
            z_matmul(1)
            policy_quantize(1)
            z_exp(0)
            channel_columns()

        def step(s):
            j, l = s - STAGE2_LAG, s - TURN_LAG
            hist_n, hist_h = divmod(s + 2, 2)
            pol_n, pol_k = divmod(s + 5, PACK)
            if 0 <= l < LAST_GROUP and l % 2 == 0:
                y_transpose(l, range(PACK))
                y_transpose(l + 1, range(PACK))
            if hist_n < R * NG and hist_h == 0:
                history_transpose(hist_n, 0)
                history_transpose(hist_n, 1)
            if 2 <= s + 1 < BANKS:
                z_matmul(s + 1)
            if 0 <= j < BANKS:
                u_matmul(j)
            if 1 <= s < BANKS:
                z_exp(s)
            if 0 <= s - 1 < BANKS:
                z_max(s - 1)
            if j - 2 == BANKS - 1:
                turn_last_group((2,))
            if 0 <= j - 2 < BANKS:
                y_affine(j - 2)
            if 0 <= j - 1 < BANKS:
                u_tanh(j - 1)
            if j - 2 == BANKS - 1:
                finish_last_group()
            if s % PACK == 2 and (s + 2) // PACK < R * NG:
                history_quantize((s + 2) // PACK, 0, 2)
            if pol_n == NG and pol_k == 2:
                policy_interleave(pol_n, 1)
            if s % PACK == 3 and NG <= (s + 1) // PACK < NG * NG:
                policy_quantize((s + 1) // PACK)
            if s % PACK == 1 and 0 <= s - 5 < BANKS:
                h_quantize((s - 5) // PACK)
            if (l + 1) % PACK == 0 and 0 <= l + 1 < LAST_GROUP:
                y_interleave((l + 1) // PACK, 0, F)
            if l % PACK == 0 and 0 <= l < LAST_GROUP:
                y_quantize(l // PACK, 0, F)
            if l % PACK == 1 and 0 <= l < LAST_GROUP:
                words_store(l // PACK)
            if l == BANKS - 2:
                words_store(LAST_GROUP // PACK)
                scales_store()
            if hist_n < R * NG:
                history_copy(hist_n, hist_h)
            if (NG <= pol_n < NG * NG and pol_k == 0) or (pol_n == NG * NG - 1 and pol_k == 2):
                policy_interleave(pol_n, pol_k // 2)
            if j - 2 == BANKS - 2:
                turn_last_group((0, 1))
            if 0 <= l < BANKS:
                y_store(l)
            if s % 2 == 0 and 2 <= s <= BANKS:
                z_gain(s // 2 - 1)

        def turn_last_group(slots):
            for l in range(LAST_GROUP, BANKS):
                y_transpose(l, slots)

        def finish_last_group():
            turn_last_group((3,))
            for work_on in (y_interleave, y_quantize):
                for h in range(2):
                    work_on(LAST_GROUP // PACK, h * HALF, (h + 1) * HALF)

        opening()
        for s in range(TURN_LAG + BANKS):
            step(s)
